import numpy as np
import ml_dtypes


def mxq(x, axis, fmt="e4m3"):
    dtype, down = {"e4m3": (ml_dtypes.float8_e4m3fn, 7), "e5m2": (ml_dtypes.float8_e5m2, 14)}[fmt]
    v = np.moveaxis(np.asarray(x, np.float32).astype(ml_dtypes.bfloat16).astype(np.float64), axis, -1)
    blocks = v.reshape(v.shape[:-1] + (-1, 32))
    amax = np.abs(blocks).max(-1, keepdims=True)
    byte = np.maximum(np.where(amax > 0, np.frexp(amax)[1] - 1 + 127, 0) - down, 1)
    scale = np.exp2(byte - 127.0)
    codes = (blocks / scale).astype(np.float32).astype(dtype).astype(np.float64)
    return np.moveaxis((codes * scale).reshape(v.shape), -1, axis)


WIDE = False


def mx_kscale(k):
    if not WIDE:
        return np.ones(k)
    levels = np.array([10, -10, 5, -5, 0])
    if k % 512:
        return np.exp2(np.random.permutation(np.resize(levels, k // 32))).repeat(32)
    a = np.empty((k // 512, 16))
    for p in range(k // 512):
        a[p, :8] = np.random.permutation(np.resize(levels, 8))
        for g in range(8):
            far = levels[np.abs(levels - a[p, g]) >= 10]
            a[p, g + 8] = far[np.random.randint(len(far))]
    return np.exp2(a.ravel()).repeat(32)


def f64(x):
    return np.asarray(x).astype(np.float64)


def striped(idx):
    return np.tile(idx.reshape(-1, 16).T, (8, 1)).astype(np.uint16)


def unstriped(offs):
    return offs[:16].T.reshape(-1).astype(np.int64)


def striped8(idx):
    return np.concatenate([x.reshape(-1, 16).T for x in idx]).astype(np.uint16)


def runs(offs, k):
    lists = np.stack([offs[16 * r : 16 * r + 16].T.reshape(-1) for r in range(8)]).astype(np.int64)
    return lists[np.arange(k) % 512 // 64]


def pack_weight(w):
    k, n = w.shape
    w = f64(np.asarray(w, np.float32).astype(ml_dtypes.bfloat16)).reshape(k // 32, 32, n)
    amax = np.abs(w).max(1)
    byte = np.clip(np.where(amax > 0, np.frexp(amax)[1] - 1 + 127 - 7, 1), 1, 254)
    scaled = (w * np.exp2(127.0 - byte)[:, None, :]).reshape(k, n).astype(np.float32)
    words = np.ascontiguousarray(scaled.reshape(k // 512, 128, 4, n).transpose(0, 1, 3, 2)).astype(ml_dtypes.float8_e4m3fn).view(np.uint8)
    return words, np.ascontiguousarray(byte.astype(np.uint8).reshape(k // 512, 16, n))


def unpack_weight(words, scales):
    g, p, n, _ = words.shape
    vals = np.ascontiguousarray(words).view(ml_dtypes.float8_e4m3fn).astype(np.float64) * np.repeat(np.exp2(scales.astype(np.float64) - 127.0), 8, axis=1)[..., None]
    return vals.transpose(0, 1, 3, 2).reshape(g * 512, n)


def sigmoid(v):
    return 1.0 / (1.0 + np.exp(-np.maximum(v, -700.0)))


K, T, S, N, H = 512, 2048, 512, 512, 512


def setup_inputs():
    n = np.random.standard_normal
    s = mx_kscale(K)[:, None]
    u = mx_kscale(H)
    packed_xT = pack_weight(n((K, T)) * s)
    return {
        "x_words": packed_xT[0],
        "x_scales": packed_xT[1],
        "w1": (n((K, H)) / np.sqrt(K) / s).astype(np.float32),
        "sl": np.random.uniform(1.5, 3.0, (H, 1)).astype(np.float32),
        "th": (0.5 * n((H, 1))).astype(np.float32),
        "gn": (np.random.uniform(0.5, 1.5, (H, 1)) * u[:, None]).astype(np.float32),
        "w2": (n((H, N)) / np.sqrt(H) / u[:, None]).astype(np.float32),
        "w3": (n((K, N)) / np.sqrt(K) / s).astype(np.float32),
        "tau": np.random.uniform(0.3, 0.9, (N, 1)).astype(np.float32),
        "offs": striped(np.random.permutation(T)[:S]),
        "n1": striped8(np.stack([np.random.permutation(S) for _ in range(8)])),
        "n2": striped8(np.stack([np.random.permutation(S) for _ in range(8)])),
        "two": striped(np.random.permutation(T)[:S]),
        "n3": striped8(np.stack([np.random.permutation(S) for _ in range(8)])),
        "n4": striped8(np.stack([np.random.permutation(S) for _ in range(8)])),
    }


def reference(x_words, x_scales, w1, sl, th, gn, w2, w3, tau, offs, n1, n2, two, n3, n4):
    x_two = unpack_weight(x_words, x_scales)[:, unstriped(two)]
    d = mxq(f64(w3), 0, "e4m3").T @ x_two
    top = d.max(axis=1, keepdims=True)
    ea = np.exp(f64(tau) * (d[np.arange(N)[:, None], runs(n3, N)] - top))
    xq = unpack_weight(x_words, x_scales)[:, unstriped(offs)]
    y = mxq(f64(w1), 0, "e4m3").T @ xq
    sg = sigmoid(f64(sl) * (y[np.arange(H)[:, None], runs(n1, H)] - f64(th)))
    z = f64(gn) * (1.5 * (y * (sg - (sg[np.arange(H)[:, None], runs(n2, H)]))))
    h = mxq(f64(w2), 0, "e4m3").T @ mxq(z, 0, "e4m3")
    return (2.0 * ea) * (h - (h[np.arange(N)[:, None], runs(n4, N)])) - (0.5 * d)

@@ -1,0 +1,242 @@
+from contextlib import ExitStack
+
+import concourse.mybir as mybir
+
+K, T, S, N, H = 512, 2048, 512, 512, 512
+FLOPS = 2 * K * H * S + 2 * H * N * S + 2 * K * N * S
+
+F32 = mybir.dt.float32
+BF16 = mybir.dt.bfloat16
+I32 = mybir.dt.int32
+U32 = mybir.dt.uint32
+U16 = mybir.dt.uint16
+U8 = mybir.dt.uint8
+FP8X4 = mybir.dt.float8_e4m3fn_x4
+ALU = mybir.AluOpType
+ACT = mybir.ActivationFunctionType
+
+P = 128
+PACK = 4
+HALF = S // 2
+LIST_COLS = S // 16
+HALF_COLS = LIST_COLS // 2
+
+
+def tile_picked_latepxbedb_none_p_kernel(
+    tc, x_words, x_scales, w1, sl, th, gn, w2, w3, tau, offs, n1, n2, two, n3, n4, out
+):
+    nc = tc.nc
+    halves = [slice(u * HALF, (u + 1) * HALF) for u in range(2)]
+    half_lists = [slice(u * HALF_COLS, (u + 1) * HALF_COLS) for u in range(2)]
+
+    with ExitStack() as ctx:
+        lists = ctx.enter_context(tc.tile_pool(name="lists", bufs=1))
+        keep = ctx.enter_context(tc.tile_pool(name="keep", bufs=1))
+        shared = ctx.enter_context(tc.tile_pool(name="shared", bufs=1))
+        psum = ctx.enter_context(tc.psum_pool(name="psum", bufs=1))
+
+        def load_list(name, src):
+            tile = lists.tile([P, LIST_COLS], U16, name=name)
+            nc.sync.dma_start(tile[:], src)
+            return tile
+
+        def load_column(name, src):
+            tile = keep.tile([P, PACK], F32, name=name)
+            nc.gpsimd.dma_start(tile[:], src.rearrange("(p t) o -> p (t o)", t=PACK))
+            return tile
+
+        def load_weight(name, src, cols):
+            tile = keep.tile([P, PACK, cols.stop - cols.start], F32, name=name)
+            nc.sync.dma_start(tile[:], src.rearrange("(p j) n -> p j n", j=PACK)[:, :, cols])
+            return tile
+
+        x_bytes = keep.tile([P, T], U8, name="x_bytes", align_bytes=64)
+        nc.vector.memset(x_bytes[:].bitcast(I32), 0)
+        for q in range(4):
+            nc.sync.dma_start(
+                x_bytes[32 * q : 32 * q + 4, :].bitcast(I32), x_scales[0, 4 * q : 4 * q + 4, :].bitcast(I32)
+            )
+        offs_sb = load_list("offs_sb", offs)
+        two_sb = load_list("two_sb", two)
+        w1_raw = [load_weight("w1_raw%d" % u, w1, halves[u]) for u in range(2)]
+        x_codes = keep.tile([P, T], U32, name="x_codes", align_bytes=64)
+        nc.sync.dma_start(x_codes[:].bitcast(I32), x_words[0].rearrange("p n t -> p (n t)").bitcast(I32))
+        w3_raw = load_weight("w3_raw", w3, slice(0, N))
+        n1_sb = load_list("n1_sb", n1)
+        n2_sb = load_list("n2_sb", n2)
+        w2_raw = load_weight("w2_raw", w2, slice(0, N))
+        n3_sb = load_list("n3_sb", n3)
+        n4_sb = load_list("n4_sb", n4)
+        sl_sb = load_column("sl_sb", sl)
+        th_sb = load_column("th_sb", th)
+        gn_sb = load_column("gn_sb", gn)
+        tau_sb = load_column("tau_sb", tau)
+
+        sig_bias = keep.tile([P, PACK], F32, name="sig_bias")
+        neg_sl = keep.tile([P, PACK], F32, name="neg_sl")
+        gain = keep.tile([P, PACK], F32, name="gain")
+        neg_tau = keep.tile([P, PACK], F32, name="neg_tau")
+        nc.gpsimd.tensor_scalar(neg_sl[:], sl_sb[:], -1.0, 0.0, ALU.mult, ALU.add)
+        nc.gpsimd.tensor_tensor(sig_bias[:], neg_sl[:], th_sb[:], ALU.mult)
+        nc.gpsimd.tensor_scalar(gain[:], gn_sb[:], 1.5, 0.0, ALU.mult, ALU.add)
+        nc.gpsimd.tensor_scalar(neg_tau[:], tau_sb[:], -1.0, 0.0, ALU.mult, ALU.add)
+
+        def tagged(name, shape, dtype, tag):
+            return keep.tile(shape, dtype, name=name, tag=tag, align_bytes=64)
+
+        def gather_bytes(name, index):
+            tile = tagged(name, [P, S], U8, name)
+            nc.vector.tensor_copy(tile[:], x_bytes[:].indirect(index[:]))
+            return tile
+
+        def gather_codes(name, index):
+            tile = tagged(name, [P, S], U32, "picked")
+            nc.vector.tensor_copy(tile[:], x_codes[:].indirect(index[:]))
+            return tile
+
+        def round_weight(copy, grouped, raw, cols):
+            members = slice(cols.start // PACK, cols.stop // PACK)
+            copy(
+                grouped[:].rearrange("p (t m j) -> p m t j", t=PACK, j=PACK)[:, members],
+                raw[:].rearrange("p j (m t) -> p m t j", t=PACK),
+            )
+
+        def quantize(codes, scales, grouped):
+            nc.vector.quantize_mx(out=codes.bitcast(FP8X4), scales=scales, in_=grouped)
+
+        def product(bank, w_codes, w_scales, codes, scales):
+            nc.tensor.matmul_mx(
+                out=bank,
+                lhsT=w_codes.bitcast(FP8X4),
+                lhsT_scale=w_scales,
+                rhs=codes.bitcast(FP8X4),
+                rhs_scale=scales,
+                start=True,
+                stop=True,
+            )
+
+        everything = slice(0, S)
+        blocks = [slice(t * P, (t + 1) * P) for t in range(PACK)]
+
+        offs_bytes = gather_bytes("offs_bytes", offs_sb)
+        two_bytes = gather_bytes("two_bytes", two_sb)
+
+        w1_bf = tagged("w1_bf", [P, PACK * H], BF16, "w1_bf")
+        for u in range(2):
+            round_weight(nc.scalar.copy, w1_bf, w1_raw[u], halves[u])
+        w1_codes = [tagged("w1_codes%d" % t, [P, P], U32, "rounded" if t == 0 else "w1_codes%d" % t) for t in range(PACK)]
+        w1_scales = tagged("w1_scales", [P, H], U8, "w1_scales")
+        for t in range(PACK):
+            quantize(w1_codes[t][:], w1_scales[:, blocks[t]], w1_bf[:, t * PACK * P : (t + 1) * PACK * P])
+        offs_codes = gather_codes("offs_codes", offs_sb)
+        y_bank = [psum.tile([P, S], F32, name="y_bank%d" % t) for t in range(PACK)]
+        for t in range(PACK):
+            product(y_bank[t][:], w1_codes[t][:], w1_scales[:, blocks[t]], offs_codes[:], offs_bytes[:])
+
+        y_sb = [shared.tile([P, S], F32, name="y_sb%d" % t, offset=4 * S * t) for t in range(PACK)]
+        sg = [keep.tile([P, S], F32, name="sg%d" % t) for t in range(PACK)]
+        sg_far = [keep.tile([P, S], F32, name="sg_far%d" % t) for t in range(PACK)]
+
+        def through(func, dst, window, index, **affine):
+            for u in range(2):
+                nc.scalar.activation(dst[:, halves[u]], window[:].indirect(index[:, half_lists[u]]), func, **affine)
+
+        def sigmoid_of(t):
+            through(ACT.Sigmoid, sg[t], y_sb[t], n1_sb, bias=sig_bias[:, t : t + 1], scale=sl_sb[:, t : t + 1])
+
+        nc.vector.tensor_copy(y_sb[0][:], y_bank[0][:])
+        w3_bf = tagged("w3_bf", [P, PACK * N], BF16, "rounded")
+        round_weight(nc.vector.tensor_copy, w3_bf, w3_raw, everything)
+        two_codes = gather_codes("two_codes", two_sb)
+        w3_codes = tagged("w3_codes", [P, N], U32, "w3_codes")
+        w3_scales = tagged("w3_scales", [P, N], U8, "w3_scales")
+        quantize(w3_codes[:], w3_scales[:], w3_bf[:])
+        nc.vector.tensor_copy(y_sb[3][:], y_bank[3][:])
+        w2_bf = tagged("w2_bf", [P, PACK * N], BF16, "rounded")
+        round_weight(nc.vector.tensor_copy, w2_bf, w2_raw, everything)
+
+        for t in range(2):
+            sigmoid_of(t)
+            nc.scalar.copy(y_sb[t + 1][:], y_bank[t + 1][:])
+            through(ACT.Copy, sg_far[t], sg[t], n2_sb)
+        for t in range(2, PACK):
+            sigmoid_of(t)
+        for t in range(2, PACK):
+            through(ACT.Copy, sg_far[t], sg[t], n2_sb)
+
+        d_sb = [keep.tile([P, S], F32, name="d_sb%d" % t) for t in range(PACK)]
+        top = keep.tile([P, PACK], F32, name="top")
+        for t in range(PACK):
+            d_bank = psum.tile([P, S], F32, name="d_bank", tag="dh_bank%d" % t)
+            product(d_bank[:], w3_codes[:, blocks[t]], w3_scales[:, blocks[t]], two_codes[:], two_bytes[:])
+            nc.vector.tensor_scalar(d_sb[t][:], d_bank[:], 1.0, None, ALU.mult, ALU.max, accum_out=top[:, t : t + 1])
+        w2_codes = tagged("w2_codes", [P, N], U32, "w2_codes")
+        w2_scales = tagged("w2_scales", [P, N], U8, "w2_scales")
+        quantize(w2_codes[:], w2_scales[:], w2_bf[:])
+        exp_bias = keep.tile([P, PACK], F32, name="exp_bias")
+        nc.gpsimd.tensor_tensor(exp_bias[:], top[:], neg_tau[:], ALU.mult)
+
+        z = keep.tile([P, PACK, S], F32, name="z")
+        for t in range(PACK):
+            diff = tagged("diff", [P, S], F32, "w3_codes" if t % 2 else "picked")
+            for u in range(2):
+                nc.vector.tensor_tensor(diff[:, halves[u]], sg[t][:, halves[u]], sg_far[t][:, halves[u]], ALU.subtract)
+            for u in range(2):
+                nc.vector.scalar_tensor_tensor(
+                    z[:, t, halves[u]], diff[:, halves[u]], gain[:, t : t + 1], y_bank[t][:, halves[u]], ALU.mult, ALU.mult
+                )
+
+        z_bf = tagged("z_bf", [P, PACK * S], BF16, "rounded")
+        z_codes = tagged("z_codes", [P, S], U32, "z_codes")
+        z_scales = tagged("z_scales", [P, S], U8, "z_scales")
+        for u in range(2):
+            nc.vector.tensor_copy(
+                z_bf[:, PACK * u * HALF : PACK * (u + 1) * HALF].rearrange("p (c i t) -> p c t i", i=4, t=PACK),
+                z[:, :, halves[u]].rearrange("p t (c i) -> p c t i", i=4),
+            )
+        for u in range(2):
+            quantize(z_codes[:, halves[u]], z_scales[:, halves[u]], z_bf[:, PACK * u * HALF : PACK * (u + 1) * HALF])
+
+        ea = shared.tile([P, PACK, S], F32, name="ea", offset=0)
+        for t in range(PACK):
+            through(ACT.Exp, ea[:, t, :], d_sb[t], n3_sb, bias=exp_bias[:, t : t + 1], scale=tau_sb[:, t : t + 1])
+
+        h_bank = [psum.tile([P, S], F32, name="h_bank%d" % t, tag="dh_bank%d" % t) for t in range(PACK)]
+        for t in range(PACK):
+            for u in range(2):
+                product(
+                    h_bank[t][:, halves[u]], w2_codes[:, blocks[t]], w2_scales[:, blocks[t]],
+                    z_codes[:, halves[u]], z_scales[:, halves[u]],
+                )
+
+        h_sb = [keep.tile([P, S], F32, name="h_sb%d" % t) for t in range(PACK)]
+        h_far = [keep.tile([P, S], F32, name="h_far%d" % t) for t in range(PACK)]
+        for t in range(2):
+            nc.vector.tensor_copy(h_sb[t][:], h_bank[t][:])
+        for u in range(2):
+            nc.vector.tensor_copy(h_far[0][:, halves[u]], h_sb[0][:].indirect(n4_sb[:, half_lists[u]]))
+        through(ACT.Copy, h_far[1], h_sb[1], n4_sb)
+        for t in range(2, PACK):
+            nc.scalar.copy(h_sb[t][:], h_bank[t][:])
+            through(ACT.Copy, h_far[t], h_sb[t], n4_sb)
+
+        out_rows = out.rearrange("(p t) n -> p t n", t=PACK)
+        for t in range(PACK):
+            gap = keep.tile([P, S], F32, name="gap%d" % t)
+            weighted = keep.tile([P, S], F32, name="weighted%d" % t)
+            result = keep.tile([P, S], F32, name="result%d" % t)
+            for u in range(2):
+                nc.vector.tensor_tensor(gap[:, halves[u]], h_bank[t][:, halves[u]], h_far[t][:, halves[u]], ALU.subtract)
+            for u in range(2):
+                nc.vector.scalar_tensor_tensor(
+                    weighted[:, halves[u]], gap[:, halves[u]], 2.0, ea[:, t, halves[u]], ALU.mult, ALU.mult
+                )
+            for u in range(2):
+                nc.vector.scalar_tensor_tensor(
+                    result[:, halves[u]], d_sb[t][:, halves[u]], -0.5, weighted[:, halves[u]], ALU.mult, ALU.add
+                )
+            if t + 1 < PACK:
+                nc.sync.dma_start(out_rows[:, t, :], result[:])
+            else:
+                for u in range(2):
+                    nc.sync.dma_start(out_rows[:, t, halves[u]], result[:, halves[u]])

@@ -42,7 +42,7 @@ def tile_picked_latepxbedb_none_p_kernel(
 
         def load_column(name, src):
             tile = keep.tile([P, PACK], F32, name=name)
-            nc.gpsimd.dma_start(tile[:], src.rearrange("(p t) o -> p (t o)", t=PACK))
+            nc.sync.dma_start(tile[:], src.rearrange("(p t) o -> p (t o)", t=PACK))
             return tile
 
         def load_weight(name, src, cols):
@@ -56,50 +56,39 @@ def tile_picked_latepxbedb_none_p_kernel(
             nc.sync.dma_start(
                 x_bytes[32 * q : 32 * q + 4, :].bitcast(I32), x_scales[0, 4 * q : 4 * q + 4, :].bitcast(I32)
             )
+        w1_raw = [load_weight("w1_raw0", w1, halves[0])]
         offs_sb = load_list("offs_sb", offs)
         two_sb = load_list("two_sb", two)
-        w1_raw = [load_weight("w1_raw%d" % u, w1, halves[u]) for u in range(2)]
+        w1_raw.append(load_weight("w1_raw1", w1, halves[1]))
         x_codes = keep.tile([P, T], U32, name="x_codes", align_bytes=64)
         nc.sync.dma_start(x_codes[:].bitcast(I32), x_words[0].rearrange("p n t -> p (n t)").bitcast(I32))
-        w3_raw = load_weight("w3_raw", w3, slice(0, N))
-        n1_sb = load_list("n1_sb", n1)
-        n2_sb = load_list("n2_sb", n2)
-        w2_raw = load_weight("w2_raw", w2, slice(0, N))
-        n3_sb = load_list("n3_sb", n3)
-        n4_sb = load_list("n4_sb", n4)
         sl_sb = load_column("sl_sb", sl)
         th_sb = load_column("th_sb", th)
+        n1_sb = load_list("n1_sb", n1)
+        w3_raw = load_weight("w3_raw", w3, slice(0, N))
+        n2_sb = load_list("n2_sb", n2)
         gn_sb = load_column("gn_sb", gn)
+        w2_raw = load_weight("w2_raw", w2, slice(0, N))
         tau_sb = load_column("tau_sb", tau)
+        n3_sb = load_list("n3_sb", n3)
+        n4_sb = load_list("n4_sb", n4)
 
-        sig_bias = keep.tile([P, PACK], F32, name="sig_bias")
-        neg_sl = keep.tile([P, PACK], F32, name="neg_sl")
         gain = keep.tile([P, PACK], F32, name="gain")
-        neg_tau = keep.tile([P, PACK], F32, name="neg_tau")
-        nc.gpsimd.tensor_scalar(neg_sl[:], sl_sb[:], -1.0, 0.0, ALU.mult, ALU.add)
-        nc.gpsimd.tensor_tensor(sig_bias[:], neg_sl[:], th_sb[:], ALU.mult)
         nc.gpsimd.tensor_scalar(gain[:], gn_sb[:], 1.5, 0.0, ALU.mult, ALU.add)
-        nc.gpsimd.tensor_scalar(neg_tau[:], tau_sb[:], -1.0, 0.0, ALU.mult, ALU.add)
 
         def tagged(name, shape, dtype, tag):
             return keep.tile(shape, dtype, name=name, tag=tag, align_bytes=64)
 
-        def gather_bytes(name, index):
-            tile = tagged(name, [P, S], U8, name)
-            nc.vector.tensor_copy(tile[:], x_bytes[:].indirect(index[:]))
+        def gather(name, dtype, table, index, tag):
+            tile = tagged(name, [P, S], dtype, tag)
+            nc.vector.tensor_copy(tile[:], table[:].indirect(index[:]))
             return tile
 
-        def gather_codes(name, index):
-            tile = tagged(name, [P, S], U32, "picked")
-            nc.vector.tensor_copy(tile[:], x_codes[:].indirect(index[:]))
-            return tile
+        def dealt(grouped, members):
+            return grouped[:].rearrange("p (t m j) -> p m t j", t=PACK, j=PACK)[:, members]
 
-        def round_weight(copy, grouped, raw, cols):
-            members = slice(cols.start // PACK, cols.stop // PACK)
-            copy(
-                grouped[:].rearrange("p (t m j) -> p m t j", t=PACK, j=PACK)[:, members],
-                raw[:].rearrange("p j (m t) -> p m t j", t=PACK),
-            )
+        def by_member(raw):
+            return raw.rearrange("p j (m t) -> p m t j", t=PACK)
 
         def quantize(codes, scales, grouped):
             nc.vector.quantize_mx(out=codes.bitcast(FP8X4), scales=scales, in_=grouped)
@@ -115,78 +104,102 @@ def tile_picked_latepxbedb_none_p_kernel(
                 stop=True,
             )
 
-        everything = slice(0, S)
         blocks = [slice(t * P, (t + 1) * P) for t in range(PACK)]
+        member_halves = [slice(u * P // 2, (u + 1) * P // 2) for u in range(2)]
 
-        offs_bytes = gather_bytes("offs_bytes", offs_sb)
-        two_bytes = gather_bytes("two_bytes", two_sb)
+        def pieces(t):
+            return halves if t == PACK - 1 else [slice(0, S)]
+
+        y_win = [shared.tile([P, 2 * S], F32, name="y_win%d" % b, offset=8 * S * b) for b in range(PACK)]
+        sg_win = [keep.tile([P, 2 * S], F32, name="sg_win%d" % t) for t in range(PACK)]
+        d_win = [keep.tile([P, 2 * S], F32, name="d_win%d" % t) for t in range(PACK)]
+        h_win = [keep.tile([P, 2 * S], F32, name="h_win%d" % t, tag="h_win%d" % t) for t in range(PACK)]
+        for tile in y_win[:2] + sg_win:
+            nc.vector.memset(tile[:, S:], 0.0)
+        for tile in y_win[2:]:
+            nc.gpsimd.memset(tile[:, S:], 0.0)
+        warm = keep.tile([P, 1], F32, name="warm")
+        nc.scalar.activation(warm[:], y_win[0][:, S : S + 1], ACT.Sigmoid)
+        y_sb = [y_win[t][:, :S] for t in range(PACK)]
+        sg = [tile[:, :S] for tile in sg_win]
+        d_sb = [tile[:, :S] for tile in d_win]
+        sg_far = [tile[:, S:] for tile in d_win]
+        h2 = [tile[:, :S] for tile in h_win]
+        diff = [tile[:, S:] for tile in h_win]
+
+        offs_bytes = gather("offs_bytes", U8, x_bytes, offs_sb, "offs_bytes")
+        two_bytes = gather("two_bytes", U8, x_bytes, two_sb, "two_bytes")
 
         w1_bf = tagged("w1_bf", [P, PACK * H], BF16, "w1_bf")
         for u in range(2):
-            round_weight(nc.scalar.copy, w1_bf, w1_raw[u], halves[u])
-        w1_codes = [tagged("w1_codes%d" % t, [P, P], U32, "rounded" if t == 0 else "w1_codes%d" % t) for t in range(PACK)]
+            nc.scalar.copy(dealt(w1_bf, member_halves[u]), by_member(w1_raw[u][:]))
+        w1_codes = [tagged("w1_codes%d" % t, [P, P], U32, "after_y%d" % t) for t in range(PACK)]
         w1_scales = tagged("w1_scales", [P, H], U8, "w1_scales")
+        y_bank = [psum.tile([P, S], F32, name="y_bank%d" % t, tag="yh_bank%d" % t) for t in range(PACK)]
         for t in range(PACK):
             quantize(w1_codes[t][:], w1_scales[:, blocks[t]], w1_bf[:, t * PACK * P : (t + 1) * PACK * P])
-        offs_codes = gather_codes("offs_codes", offs_sb)
-        y_bank = [psum.tile([P, S], F32, name="y_bank%d" % t) for t in range(PACK)]
+        offs_codes = tagged("offs_codes", [P, S], U32, "offs_codes")
+        for u in range(2):
+            nc.vector.tensor_copy(offs_codes[:, halves[u]], x_codes[:].indirect(offs_sb[:, half_lists[u]]))
+        sig_bias = keep.tile([P, PACK], F32, name="sig_bias")
+        nc.vector.scalar_tensor_tensor(sig_bias[:], sl_sb[:], -1.0, th_sb[:], ALU.mult, ALU.mult)
+        two_codes = gather("two_codes", U32, x_codes, two_sb, "two_codes")
         for t in range(PACK):
-            product(y_bank[t][:], w1_codes[t][:], w1_scales[:, blocks[t]], offs_codes[:], offs_bytes[:])
+            for cols in halves if t == 0 else [slice(0, S)]:
+                product(y_bank[t][:, cols], w1_codes[t][:], w1_scales[:, blocks[t]], offs_codes[:, cols], offs_bytes[:, cols])
 
-        y_sb = [shared.tile([P, S], F32, name="y_sb%d" % t, offset=4 * S * t) for t in range(PACK)]
-        sg = [keep.tile([P, S], F32, name="sg%d" % t) for t in range(PACK)]
-        sg_far = [keep.tile([P, S], F32, name="sg_far%d" % t) for t in range(PACK)]
-
-        def through(func, dst, window, index, **affine):
-            for u in range(2):
-                nc.scalar.activation(dst[:, halves[u]], window[:].indirect(index[:, half_lists[u]]), func, **affine)
-
-        def sigmoid_of(t):
-            through(ACT.Sigmoid, sg[t], y_sb[t], n1_sb, bias=sig_bias[:, t : t + 1], scale=sl_sb[:, t : t + 1])
-
-        nc.vector.tensor_copy(y_sb[0][:], y_bank[0][:])
-        w3_bf = tagged("w3_bf", [P, PACK * N], BF16, "rounded")
-        round_weight(nc.vector.tensor_copy, w3_bf, w3_raw, everything)
-        two_codes = gather_codes("two_codes", two_sb)
         w3_codes = tagged("w3_codes", [P, N], U32, "w3_codes")
         w3_scales = tagged("w3_scales", [P, N], U8, "w3_scales")
+
+        def through(func, dst, window, index, **affine):
+            nc.scalar.activation(dst, window[:].indirect(index[:]), func, **affine)
+
+        def fetch_in_halves(dst, window, index):
+            for u in range(2):
+                nc.scalar.activation(dst[:, halves[u]], window[:].indirect(index[:, half_lists[u]]), ACT.Copy)
+
+        def sigmoid_of(t):
+            through(ACT.Sigmoid, sg[t], y_win[t], n1_sb, bias=sig_bias[:, t : t + 1], scale=sl_sb[:, t : t + 1])
+
+        nc.scalar.copy(y_sb[0], y_bank[0][:])
+        nc.vector.tensor_copy(y_sb[1], y_bank[1][:])
+        sigmoid_of(0)
+        sigmoid_of(1)
+        w3_bf = tagged("w3_bf", [P, PACK * N], BF16, "after_y1")
+        nc.vector.tensor_copy(dealt(w3_bf, slice(0, P)), by_member(w3_raw[:]))
+        nc.vector.tensor_copy(y_sb[2], y_bank[2][:])
         quantize(w3_codes[:], w3_scales[:], w3_bf[:])
-        nc.vector.tensor_copy(y_sb[3][:], y_bank[3][:])
-        w2_bf = tagged("w2_bf", [P, PACK * N], BF16, "rounded")
-        round_weight(nc.vector.tensor_copy, w2_bf, w2_raw, everything)
+        nc.vector.tensor_copy(y_sb[3], y_bank[3][:])
+        sigmoid_of(2)
+        through(ACT.Copy, sg_far[0], sg_win[0], n2_sb)
+        sigmoid_of(3)
+        for t in range(1, PACK - 1):
+            through(ACT.Copy, sg_far[t], sg_win[t], n2_sb)
+        fetch_in_halves(sg_far[3], sg_win[3], n2_sb)
+        w2_bf = tagged("w2_bf", [P, PACK * N], BF16, "after_y1")
+        nc.vector.tensor_copy(dealt(w2_bf, slice(0, P)), by_member(w2_raw[:]))
 
-        for t in range(2):
-            sigmoid_of(t)
-            nc.scalar.copy(y_sb[t + 1][:], y_bank[t + 1][:])
-            through(ACT.Copy, sg_far[t], sg[t], n2_sb)
-        for t in range(2, PACK):
-            sigmoid_of(t)
-        for t in range(2, PACK):
-            through(ACT.Copy, sg_far[t], sg[t], n2_sb)
-
-        d_sb = [keep.tile([P, S], F32, name="d_sb%d" % t) for t in range(PACK)]
-        top = keep.tile([P, PACK], F32, name="top")
+        d_bank = [psum.tile([P, S], F32, name="d_bank%d" % t) for t in range(PACK)]
+        top = tagged("top", [P, PACK], F32, "top")
         for t in range(PACK):
-            d_bank = psum.tile([P, S], F32, name="d_bank", tag="dh_bank%d" % t)
-            product(d_bank[:], w3_codes[:, blocks[t]], w3_scales[:, blocks[t]], two_codes[:], two_bytes[:])
-            nc.vector.tensor_scalar(d_sb[t][:], d_bank[:], 1.0, None, ALU.mult, ALU.max, accum_out=top[:, t : t + 1])
+            product(d_bank[t][:], w3_codes[:, blocks[t]], w3_scales[:, blocks[t]], two_codes[:], two_bytes[:])
+            nc.vector.tensor_scalar(d_sb[t], d_bank[t][:], 1.0, None, ALU.mult, ALU.max, accum_out=top[:, t : t + 1])
         w2_codes = tagged("w2_codes", [P, N], U32, "w2_codes")
         w2_scales = tagged("w2_scales", [P, N], U8, "w2_scales")
         quantize(w2_codes[:], w2_scales[:], w2_bf[:])
         exp_bias = keep.tile([P, PACK], F32, name="exp_bias")
-        nc.gpsimd.tensor_tensor(exp_bias[:], top[:], neg_tau[:], ALU.mult)
+        nc.vector.scalar_tensor_tensor(exp_bias[:], top[:], -1.0, tau_sb[:], ALU.mult, ALU.mult)
 
-        z = keep.tile([P, PACK, S], F32, name="z")
+        z = tagged("z", [P, PACK, S], F32, "top")
         for t in range(PACK):
-            diff = tagged("diff", [P, S], F32, "w3_codes" if t % 2 else "picked")
-            for u in range(2):
-                nc.vector.tensor_tensor(diff[:, halves[u]], sg[t][:, halves[u]], sg_far[t][:, halves[u]], ALU.subtract)
-            for u in range(2):
+            for cols in pieces(t):
+                nc.gpsimd.tensor_tensor(diff[t][:, cols], sg[t][:, cols], sg_far[t][:, cols], ALU.subtract)
+            for cols in pieces(t):
                 nc.vector.scalar_tensor_tensor(
-                    z[:, t, halves[u]], diff[:, halves[u]], gain[:, t : t + 1], y_bank[t][:, halves[u]], ALU.mult, ALU.mult
+                    z[:, t, cols], diff[t][:, cols], gain[:, t : t + 1], y_bank[t][:, cols], ALU.mult, ALU.mult
                 )
 
-        z_bf = tagged("z_bf", [P, PACK * S], BF16, "rounded")
+        z_bf = tagged("z_bf", [P, PACK * S], BF16, "after_y1")
         z_codes = tagged("z_codes", [P, S], U32, "z_codes")
         z_scales = tagged("z_scales", [P, S], U8, "z_scales")
         for u in range(2):
@@ -197,11 +210,14 @@ def tile_picked_latepxbedb_none_p_kernel(
         for u in range(2):
             quantize(z_codes[:, halves[u]], z_scales[:, halves[u]], z_bf[:, PACK * u * HALF : PACK * (u + 1) * HALF])
 
-        ea = shared.tile([P, PACK, S], F32, name="ea", offset=0)
-        for t in range(PACK):
-            through(ACT.Exp, ea[:, t, :], d_sb[t], n3_sb, bias=exp_bias[:, t : t + 1], scale=tau_sb[:, t : t + 1])
+        def exp_of(t, dst):
+            through(ACT.Exp, dst, d_win[t], n3_sb, bias=exp_bias[:, t : t + 1], scale=tau_sb[:, t : t + 1])
+            return dst
 
-        h_bank = [psum.tile([P, S], F32, name="h_bank%d" % t, tag="dh_bank%d" % t) for t in range(PACK)]
+        ea_early = shared.tile([P, PACK - 1, S], F32, name="ea_early", offset=8 * S * 2)
+        ea = [exp_of(t, ea_early[:, t, :]) for t in range(PACK - 1)]
+
+        h_bank = [psum.tile([P, S], F32, name="h_bank%d" % t, tag="yh_bank%d" % t) for t in range(PACK)]
         for t in range(PACK):
             for u in range(2):
                 product(
@@ -209,34 +225,43 @@ def tile_picked_latepxbedb_none_p_kernel(
                     z_codes[:, halves[u]], z_scales[:, halves[u]],
                 )
 
-        h_sb = [keep.tile([P, S], F32, name="h_sb%d" % t) for t in range(PACK)]
-        h_far = [keep.tile([P, S], F32, name="h_far%d" % t) for t in range(PACK)]
-        for t in range(2):
-            nc.vector.tensor_copy(h_sb[t][:], h_bank[t][:])
-        for u in range(2):
-            nc.vector.tensor_copy(h_far[0][:, halves[u]], h_sb[0][:].indirect(n4_sb[:, half_lists[u]]))
-        through(ACT.Copy, h_far[1], h_sb[1], n4_sb)
-        for t in range(2, PACK):
-            nc.scalar.copy(h_sb[t][:], h_bank[t][:])
-            through(ACT.Copy, h_far[t], h_sb[t], n4_sb)
+        h2_far = [keep.tile([P, S], F32, name="h2_far%d" % t) for t in range(PACK)]
+        for t in range(PACK):
+            nc.vector.tensor_scalar(h2[t], h_bank[t][:], 2.0, None, ALU.mult)
+        for t in range(PACK - 1):
+            through(ACT.Copy, h2_far[t][:], h_win[t], n4_sb)
+        ea_last = keep.tile([P, S], F32, name="ea_last", tag="h_win1")
+        ea.append(exp_of(PACK - 1, ea_last[:]))
+        fetch_in_halves(h2_far[3], h_win[3], n4_sb)
 
         out_rows = out.rearrange("(p t) n -> p t n", t=PACK)
-        for t in range(PACK):
-            gap = keep.tile([P, S], F32, name="gap%d" % t)
-            weighted = keep.tile([P, S], F32, name="weighted%d" % t)
-            result = keep.tile([P, S], F32, name="result%d" % t)
-            for u in range(2):
-                nc.vector.tensor_tensor(gap[:, halves[u]], h_bank[t][:, halves[u]], h_far[t][:, halves[u]], ALU.subtract)
-            for u in range(2):
+        gap = {}
+        weighted = {}
+        result = [keep.tile([P, S], F32, name="result%d" % t) for t in range(PACK)]
+
+        def start_of(t):
+            gap[t] = keep.tile([P, S], F32, name="gap", tag="gap%d" % t if t < 3 else "weighted1")
+            weighted[t] = keep.tile([P, S], F32, name="weighted", tag="weighted%d" % t)
+            for cols in pieces(t):
                 nc.vector.scalar_tensor_tensor(
-                    weighted[:, halves[u]], gap[:, halves[u]], 2.0, ea[:, t, halves[u]], ALU.mult, ALU.mult
+                    gap[t][:, cols], h_bank[t][:, cols], 2.0, h2_far[t][:, cols], ALU.mult, ALU.subtract
                 )
-            for u in range(2):
+            engine = nc.vector if t == PACK - 1 else nc.gpsimd
+            for cols in pieces(t):
+                engine.tensor_tensor(weighted[t][:, cols], gap[t][:, cols], ea[t][:, cols], ALU.mult)
+
+        def end_of(t):
+            for cols in pieces(t):
                 nc.vector.scalar_tensor_tensor(
-                    result[:, halves[u]], d_sb[t][:, halves[u]], -0.5, weighted[:, halves[u]], ALU.mult, ALU.add
+                    result[t][:, cols], d_bank[t][:, cols], -0.5, weighted[t][:, cols], ALU.mult, ALU.add
                 )
-            if t + 1 < PACK:
-                nc.sync.dma_start(out_rows[:, t, :], result[:])
-            else:
-                for u in range(2):
-                    nc.sync.dma_start(out_rows[:, t, halves[u]], result[:, halves[u]])
+                nc.sync.dma_start(out_rows[:, t, cols], result[t][:, cols])
+
+        start_of(0)
+        start_of(1)
+        end_of(0)
+        start_of(2)
+        end_of(1)
+        start_of(3)
+        end_of(2)
+        end_of(3)

@@ -232,36 +232,43 @@ def tile_picked_latepxbedb_none_p_kernel(
             through(ACT.Copy, h2_far[t][:], h_win[t], n4_sb)
         ea_last = keep.tile([P, S], F32, name="ea_last", tag="h_win1")
         ea.append(exp_of(PACK - 1, ea_last[:]))
-        fetch_in_halves(h2_far[3], h_win[3], n4_sb)
+        last = PACK - 1
+        nc.scalar.activation(h2_far[last][:, halves[1]], h_win[last][:].indirect(n4_sb[:, half_lists[1]]), ACT.Copy)
 
         out_rows = out.rearrange("(p t) n -> p t n", t=PACK)
-        gap = {}
-        weighted = {}
+        gap = [keep.tile([P, S], F32, name="gap%d" % t) for t in range(last)]
+        weighted = [keep.tile([P, S], F32, name="weighted%d" % t, tag="weighted%d" % t) for t in range(PACK)]
         result = [keep.tile([P, S], F32, name="result%d" % t) for t in range(PACK)]
+        everything = slice(0, S)
 
-        def start_of(t):
-            gap[t] = keep.tile([P, S], F32, name="gap", tag="gap%d" % t if t < 3 else "weighted1")
-            weighted[t] = keep.tile([P, S], F32, name="weighted", tag="weighted%d" % t)
-            for cols in pieces(t):
-                nc.vector.scalar_tensor_tensor(
-                    gap[t][:, cols], h_bank[t][:, cols], 2.0, h2_far[t][:, cols], ALU.mult, ALU.subtract
-                )
-            engine = nc.vector if t == PACK - 1 else nc.gpsimd
-            for cols in pieces(t):
-                engine.tensor_tensor(weighted[t][:, cols], gap[t][:, cols], ea[t][:, cols], ALU.mult)
+        def gap_of(t, dst, cols):
+            nc.vector.scalar_tensor_tensor(dst, h_bank[t][:, cols], 2.0, h2_far[t][:, cols], ALU.mult, ALU.subtract)
 
-        def end_of(t):
-            for cols in pieces(t):
-                nc.vector.scalar_tensor_tensor(
-                    result[t][:, cols], d_bank[t][:, cols], -0.5, weighted[t][:, cols], ALU.mult, ALU.add
-                )
-                nc.sync.dma_start(out_rows[:, t, cols], result[t][:, cols])
+        def start(t):
+            gap_of(t, gap[t][:], everything)
+            nc.gpsimd.tensor_tensor(weighted[t][:], gap[t][:], ea[t], ALU.mult)
 
-        start_of(0)
-        start_of(1)
-        end_of(0)
-        start_of(2)
-        end_of(1)
-        start_of(3)
-        end_of(2)
-        end_of(3)
+        def weigh_last(src, cols):
+            nc.vector.tensor_tensor(weighted[last][:, cols], src, ea[last][:, cols], ALU.mult)
+
+        def finish(t, cols):
+            nc.vector.scalar_tensor_tensor(
+                result[t][:, cols], d_bank[t][:, cols], -0.5, weighted[t][:, cols], ALU.mult, ALU.add
+            )
+            nc.sync.dma_start(out_rows[:, t, cols], result[t][:, cols])
+
+        start(0)
+        nc.vector.tensor_copy(h2_far[last][:, halves[0]], h_win[last][:].indirect(n4_sb[:, half_lists[0]]))
+        start(1)
+        gap_first = keep.tile([P, HALF], F32, name="gap_first")
+        gap_of(last, gap_first[:], halves[0])
+        finish(0, everything)
+        start(2)
+        finish(1, everything)
+        weigh_last(gap_first[:], halves[0])
+        gap_second = keep.tile([P, HALF], F32, name="gap_second", tag="weighted1")
+        gap_of(last, gap_second[:], halves[1])
+        finish(last, halves[0])
+        weigh_last(gap_second[:], halves[1])
+        finish(2, everything)
+        finish(last, halves[1])

from contextlib import ExitStack

import concourse.mybir as mybir

K, T, S, N, H = 512, 2048, 512, 512, 512
FLOPS = 2 * K * H * S + 2 * H * N * S + 2 * K * N * S

F32 = mybir.dt.float32
BF16 = mybir.dt.bfloat16
I32 = mybir.dt.int32
U32 = mybir.dt.uint32
U16 = mybir.dt.uint16
U8 = mybir.dt.uint8
FP8X4 = mybir.dt.float8_e4m3fn_x4
ALU = mybir.AluOpType
ACT = mybir.ActivationFunctionType

P = 128
PACK = 4
HALF = S // 2
LIST_COLS = S // 16
HALF_COLS = LIST_COLS // 2


def tile_picked_latepxbedb_none_p_kernel(
    tc, x_words, x_scales, w1, sl, th, gn, w2, w3, tau, offs, n1, n2, two, n3, n4, out
):
    nc = tc.nc
    halves = [slice(u * HALF, (u + 1) * HALF) for u in range(2)]
    half_lists = [slice(u * HALF_COLS, (u + 1) * HALF_COLS) for u in range(2)]

    with ExitStack() as ctx:
        lists = ctx.enter_context(tc.tile_pool(name="lists", bufs=1))
        keep = ctx.enter_context(tc.tile_pool(name="keep", bufs=1))
        shared = ctx.enter_context(tc.tile_pool(name="shared", bufs=1))
        psum = ctx.enter_context(tc.psum_pool(name="psum", bufs=1))

        def load_list(name, src):
            tile = lists.tile([P, LIST_COLS], U16, name=name)
            nc.sync.dma_start(tile[:], src)
            return tile

        def load_column(name, src):
            tile = keep.tile([P, PACK], F32, name=name)
            nc.sync.dma_start(tile[:], src.rearrange("(p t) o -> p (t o)", t=PACK))
            return tile

        def load_weight(name, src, cols):
            tile = keep.tile([P, PACK, cols.stop - cols.start], F32, name=name)
            nc.sync.dma_start(tile[:], src.rearrange("(p j) n -> p j n", j=PACK)[:, :, cols])
            return tile

        x_bytes = keep.tile([P, T], U8, name="x_bytes", align_bytes=64)
        nc.vector.memset(x_bytes[:].bitcast(I32), 0)
        for q in range(4):
            nc.sync.dma_start(
                x_bytes[32 * q : 32 * q + 4, :].bitcast(I32), x_scales[0, 4 * q : 4 * q + 4, :].bitcast(I32)
            )
        w1_raw = [load_weight("w1_raw0", w1, halves[0])]
        offs_sb = load_list("offs_sb", offs)
        two_sb = load_list("two_sb", two)
        w1_raw.append(load_weight("w1_raw1", w1, halves[1]))
        x_codes = keep.tile([P, T], U32, name="x_codes", align_bytes=64)
        nc.sync.dma_start(x_codes[:].bitcast(I32), x_words[0].rearrange("p n t -> p (n t)").bitcast(I32))
        sl_sb = load_column("sl_sb", sl)
        th_sb = load_column("th_sb", th)
        n1_sb = load_list("n1_sb", n1)
        w3_raw = load_weight("w3_raw", w3, slice(0, N))
        n2_sb = load_list("n2_sb", n2)
        gn_sb = load_column("gn_sb", gn)
        w2_raw = load_weight("w2_raw", w2, slice(0, N))
        tau_sb = load_column("tau_sb", tau)
        n3_sb = load_list("n3_sb", n3)
        n4_sb = load_list("n4_sb", n4)

        gain = keep.tile([P, PACK], F32, name="gain")
        nc.gpsimd.tensor_scalar(gain[:], gn_sb[:], 1.5, 0.0, ALU.mult, ALU.add)

        def tagged(name, shape, dtype, tag):
            return keep.tile(shape, dtype, name=name, tag=tag, align_bytes=64)

        def gather(name, dtype, table, index, tag):
            tile = tagged(name, [P, S], dtype, tag)
            nc.vector.tensor_copy(tile[:], table[:].indirect(index[:]))
            return tile

        def dealt(grouped, members):
            return grouped[:].rearrange("p (t m j) -> p m t j", t=PACK, j=PACK)[:, members]

        def by_member(raw):
            return raw.rearrange("p j (m t) -> p m t j", t=PACK)

        def quantize(codes, scales, grouped):
            nc.vector.quantize_mx(out=codes.bitcast(FP8X4), scales=scales, in_=grouped)

        def product(bank, w_codes, w_scales, codes, scales):
            nc.tensor.matmul_mx(
                out=bank,
                lhsT=w_codes.bitcast(FP8X4),
                lhsT_scale=w_scales,
                rhs=codes.bitcast(FP8X4),
                rhs_scale=scales,
                start=True,
                stop=True,
            )

        blocks = [slice(t * P, (t + 1) * P) for t in range(PACK)]
        member_halves = [slice(u * P // 2, (u + 1) * P // 2) for u in range(2)]

        def pieces(t):
            return halves if t == PACK - 1 else [slice(0, S)]

        y_win = [shared.tile([P, 2 * S], F32, name="y_win%d" % b, offset=8 * S * b) for b in range(PACK)]
        sg_win = [keep.tile([P, 2 * S], F32, name="sg_win%d" % t) for t in range(PACK)]
        d_win = [keep.tile([P, 2 * S], F32, name="d_win%d" % t) for t in range(PACK)]
        h_win = [keep.tile([P, 2 * S], F32, name="h_win%d" % t, tag="h_win%d" % t) for t in range(PACK)]
        for tile in y_win[:2] + sg_win:
            nc.vector.memset(tile[:, S:], 0.0)
        for tile in y_win[2:]:
            nc.gpsimd.memset(tile[:, S:], 0.0)
        warm = keep.tile([P, 1], F32, name="warm")
        nc.scalar.activation(warm[:], y_win[0][:, S : S + 1], ACT.Sigmoid)
        y_sb = [y_win[t][:, :S] for t in range(PACK)]
        sg = [tile[:, :S] for tile in sg_win]
        d_sb = [tile[:, :S] for tile in d_win]
        sg_far = [tile[:, S:] for tile in d_win]
        h2 = [tile[:, :S] for tile in h_win]
        diff = [tile[:, S:] for tile in h_win]

        offs_bytes = gather("offs_bytes", U8, x_bytes, offs_sb, "offs_bytes")
        two_bytes = gather("two_bytes", U8, x_bytes, two_sb, "two_bytes")

        w1_bf = tagged("w1_bf", [P, PACK * H], BF16, "w1_bf")
        for u in range(2):
            nc.scalar.copy(dealt(w1_bf, member_halves[u]), by_member(w1_raw[u][:]))
        w1_codes = [tagged("w1_codes%d" % t, [P, P], U32, "after_y%d" % t) for t in range(PACK)]
        w1_scales = tagged("w1_scales", [P, H], U8, "w1_scales")
        y_bank = [psum.tile([P, S], F32, name="y_bank%d" % t, tag="yh_bank%d" % t) for t in range(PACK)]
        for t in range(PACK):
            quantize(w1_codes[t][:], w1_scales[:, blocks[t]], w1_bf[:, t * PACK * P : (t + 1) * PACK * P])
        offs_codes = tagged("offs_codes", [P, S], U32, "offs_codes")
        for u in range(2):
            nc.vector.tensor_copy(offs_codes[:, halves[u]], x_codes[:].indirect(offs_sb[:, half_lists[u]]))
        sig_bias = keep.tile([P, PACK], F32, name="sig_bias")
        nc.vector.scalar_tensor_tensor(sig_bias[:], sl_sb[:], -1.0, th_sb[:], ALU.mult, ALU.mult)
        two_codes = gather("two_codes", U32, x_codes, two_sb, "two_codes")
        for t in range(PACK):
            for cols in halves if t == 0 else [slice(0, S)]:
                product(y_bank[t][:, cols], w1_codes[t][:], w1_scales[:, blocks[t]], offs_codes[:, cols], offs_bytes[:, cols])

        w3_codes = tagged("w3_codes", [P, N], U32, "w3_codes")
        w3_scales = tagged("w3_scales", [P, N], U8, "w3_scales")

        def through(func, dst, window, index, **affine):
            nc.scalar.activation(dst, window[:].indirect(index[:]), func, **affine)

        def fetch_in_halves(dst, window, index):
            for u in range(2):
                nc.scalar.activation(dst[:, halves[u]], window[:].indirect(index[:, half_lists[u]]), ACT.Copy)

        def sigmoid_of(t):
            through(ACT.Sigmoid, sg[t], y_win[t], n1_sb, bias=sig_bias[:, t : t + 1], scale=sl_sb[:, t : t + 1])

        nc.scalar.copy(y_sb[0], y_bank[0][:])
        nc.vector.tensor_copy(y_sb[1], y_bank[1][:])
        sigmoid_of(0)
        sigmoid_of(1)
        w3_bf = tagged("w3_bf", [P, PACK * N], BF16, "after_y1")
        nc.vector.tensor_copy(dealt(w3_bf, slice(0, P)), by_member(w3_raw[:]))
        nc.vector.tensor_copy(y_sb[2], y_bank[2][:])
        quantize(w3_codes[:], w3_scales[:], w3_bf[:])
        nc.vector.tensor_copy(y_sb[3], y_bank[3][:])
        sigmoid_of(2)
        through(ACT.Copy, sg_far[0], sg_win[0], n2_sb)
        sigmoid_of(3)
        for t in range(1, PACK - 1):
            through(ACT.Copy, sg_far[t], sg_win[t], n2_sb)
        fetch_in_halves(sg_far[3], sg_win[3], n2_sb)
        w2_bf = tagged("w2_bf", [P, PACK * N], BF16, "after_y1")
        nc.vector.tensor_copy(dealt(w2_bf, slice(0, P)), by_member(w2_raw[:]))

        d_bank = [psum.tile([P, S], F32, name="d_bank%d" % t) for t in range(PACK)]
        top = tagged("top", [P, PACK], F32, "top")
        for t in range(PACK):
            product(d_bank[t][:], w3_codes[:, blocks[t]], w3_scales[:, blocks[t]], two_codes[:], two_bytes[:])
            nc.vector.tensor_scalar(d_sb[t], d_bank[t][:], 1.0, None, ALU.mult, ALU.max, accum_out=top[:, t : t + 1])
        w2_codes = tagged("w2_codes", [P, N], U32, "w2_codes")
        w2_scales = tagged("w2_scales", [P, N], U8, "w2_scales")
        quantize(w2_codes[:], w2_scales[:], w2_bf[:])
        exp_bias = keep.tile([P, PACK], F32, name="exp_bias")
        nc.vector.scalar_tensor_tensor(exp_bias[:], top[:], -1.0, tau_sb[:], ALU.mult, ALU.mult)

        z = tagged("z", [P, PACK, S], F32, "top")
        for t in range(PACK):
            for cols in pieces(t):
                nc.gpsimd.tensor_tensor(diff[t][:, cols], sg[t][:, cols], sg_far[t][:, cols], ALU.subtract)
            for cols in pieces(t):
                nc.vector.scalar_tensor_tensor(
                    z[:, t, cols], diff[t][:, cols], gain[:, t : t + 1], y_bank[t][:, cols], ALU.mult, ALU.mult
                )

        z_bf = tagged("z_bf", [P, PACK * S], BF16, "after_y1")
        z_codes = tagged("z_codes", [P, S], U32, "z_codes")
        z_scales = tagged("z_scales", [P, S], U8, "z_scales")
        for u in range(2):
            nc.vector.tensor_copy(
                z_bf[:, PACK * u * HALF : PACK * (u + 1) * HALF].rearrange("p (c i t) -> p c t i", i=4, t=PACK),
                z[:, :, halves[u]].rearrange("p t (c i) -> p c t i", i=4),
            )
        for u in range(2):
            quantize(z_codes[:, halves[u]], z_scales[:, halves[u]], z_bf[:, PACK * u * HALF : PACK * (u + 1) * HALF])

        def exp_of(t, dst):
            through(ACT.Exp, dst, d_win[t], n3_sb, bias=exp_bias[:, t : t + 1], scale=tau_sb[:, t : t + 1])
            return dst

        ea_early = shared.tile([P, PACK - 1, S], F32, name="ea_early", offset=8 * S * 2)
        ea = [exp_of(t, ea_early[:, t, :]) for t in range(PACK - 1)]

        h_bank = [psum.tile([P, S], F32, name="h_bank%d" % t, tag="yh_bank%d" % t) for t in range(PACK)]
        for t in range(PACK):
            for u in range(2):
                product(
                    h_bank[t][:, halves[u]], w2_codes[:, blocks[t]], w2_scales[:, blocks[t]],
                    z_codes[:, halves[u]], z_scales[:, halves[u]],
                )

        h2_far = [keep.tile([P, S], F32, name="h2_far%d" % t) for t in range(PACK)]
        for t in range(PACK):
            nc.vector.tensor_scalar(h2[t], h_bank[t][:], 2.0, None, ALU.mult)
        for t in range(PACK - 1):
            through(ACT.Copy, h2_far[t][:], h_win[t], n4_sb)
        ea_last = keep.tile([P, S], F32, name="ea_last", tag="h_win1")
        ea.append(exp_of(PACK - 1, ea_last[:]))
        last = PACK - 1
        nc.scalar.activation(h2_far[last][:, halves[1]], h_win[last][:].indirect(n4_sb[:, half_lists[1]]), ACT.Copy)

        out_rows = out.rearrange("(p t) n -> p t n", t=PACK)
        gap = [keep.tile([P, S], F32, name="gap%d" % t) for t in range(last)]
        weighted = [keep.tile([P, S], F32, name="weighted%d" % t, tag="weighted%d" % t) for t in range(PACK)]
        result = [keep.tile([P, S], F32, name="result%d" % t) for t in range(PACK)]
        everything = slice(0, S)

        def gap_of(t, dst, cols):
            nc.vector.scalar_tensor_tensor(dst, h_bank[t][:, cols], 2.0, h2_far[t][:, cols], ALU.mult, ALU.subtract)

        def start(t):
            gap_of(t, gap[t][:], everything)
            nc.gpsimd.tensor_tensor(weighted[t][:], gap[t][:], ea[t], ALU.mult)

        def weigh_last(src, cols):
            nc.vector.tensor_tensor(weighted[last][:, cols], src, ea[last][:, cols], ALU.mult)

        def finish(t, cols):
            nc.vector.scalar_tensor_tensor(
                result[t][:, cols], d_bank[t][:, cols], -0.5, weighted[t][:, cols], ALU.mult, ALU.add
            )
            nc.sync.dma_start(out_rows[:, t, cols], result[t][:, cols])

        start(0)
        nc.vector.tensor_copy(h2_far[last][:, halves[0]], h_win[last][:].indirect(n4_sb[:, half_lists[0]]))
        start(1)
        gap_first = keep.tile([P, HALF], F32, name="gap_first")
        gap_of(last, gap_first[:], halves[0])
        finish(0, everything)
        start(2)
        finish(1, everything)
        weigh_last(gap_first[:], halves[0])
        gap_second = keep.tile([P, HALF], F32, name="gap_second", tag="weighted1")
        gap_of(last, gap_second[:], halves[1])
        finish(last, halves[0])
        weigh_last(gap_second[:], halves[1])
        finish(2, everything)
        finish(last, halves[1])
